import numpy as np, ml_dtypes
CORES = [34,162,290,418,42,426]
N = 6
NP, TK = 3, 512
def setup_inputs(rng):
    return {"x": rng.standard_normal((N, 128, TK), dtype=np.float32).astype(ml_dtypes.bfloat16), "w1": (rng.standard_normal((N, 128, 128), dtype=np.float32) / 8).astype(ml_dtypes.bfloat16), "w2": (rng.standard_normal((N, 128, NP * 128), dtype=np.float32) / 8).astype(ml_dtypes.bfloat16)}
def setup_inputs_big(rng):
    d = setup_inputs(rng)
    for k in ("x", "w1", "w2"): d[k] = (d[k].astype(np.float32) * 1024.0).astype(d[k].dtype)
    return d
def setup_inputs_small(rng):
    d = setup_inputs(rng)
    for k in ("x", "w1", "w2"): d[k] = (d[k].astype(np.float32) * (1 / 1024.0)).astype(d[k].dtype)
    return d
def setup_inputs_apart(rng):
    d = setup_inputs(rng)
    f = (10.0 ** rng.permutation(np.linspace(-1.5, 1.5, N))).astype(np.float32).reshape(N, 1, 1)
    for k in ("x", "w1", "w2"): d[k] = (d[k].astype(np.float32) * f).astype(d[k].dtype)
    return d
def reference(x, w1, w2):
    X, W1, W2 = x.astype(np.float64), w1.astype(np.float64), w2.astype(np.float64)
    h = [np.maximum(W1[p].T @ X[p], 0.0) for p in range(NP)]
    y = np.full((N, 128, TK), np.nan)
    for q in range(NP, N):
        y[q] = sum(W2[q][:, 128 * p:128 * p + 128].T @ h[p] for p in range(NP))
    return {"y": y.astype(ml_dtypes.bfloat16 if x.dtype != np.float64 else np.float64)}

@@ -1,0 +1,121 @@
+from concourse.bass import DstId, RemoteDMATransfer
+from concourse.mybir import AluOpType
+
+NP_, TK, D = 3, 512, 128
+NR = 2
+RW = TK // NR
+
+SCRATCH = {
+    "xs": ("sbuf", [D, TK], "bfloat16"),
+    "w1s": ("sbuf", [D, D], "bfloat16"),
+    "w2s": ("sbuf", [D, NP_ * D], "bfloat16"),
+    "zero": ("sbuf", [D, RW], "bfloat16"),
+    "ys": ("sbuf", [D, TK], "bfloat16"),
+}
+for _p in range(NP_):
+    SCRATCH["l%d" % _p] = ("sbuf", [D, TK], "bfloat16")
+for _k in range(NR):
+    SCRATCH["pb%d" % _k] = ("psum", [D, 512], "float32")
+
+SEMAPHORES = ["ld", "z", "sent"]
+SEMAPHORES += ["mm%d" % _k for _k in range(NR)] + ["v%d" % _k for _k in range(NR)] + ["st%d" % _k for _k in range(NR)]
+SEMAPHORES += ["s%d_%d" % (_p, _k) for _p in range(NP_) for _k in range(NR)]
+
+
+def _plan(cores, topo):
+    P, Q = cores[:NP_], cores[NP_:]
+    first, direct, second = [], [], []
+    for p, src in enumerate(P):
+        near = [q for q in Q if topo.may_write(src, q)]
+        far = [q for q in Q if not topo.may_write(src, q)]
+        if near:
+            direct.append((p, 0, NR, src, near))
+        if far:
+            relays = [r for r in P if r != src and topo.may_write(src, r) and all(topo.may_write(r, q) for q in far)]
+            for k in range(NR):
+                r = relays[k * len(relays) // NR]
+                first.append((p, k, k + 1, src, [r]))
+                second.append((p, k, k + 1, r, far))
+    return first + direct + second
+
+
+def _mask(topo, src, dsts):
+    m = topo.mask(src, dsts[0])
+    for d in dsts[1:]:
+        m &= topo.mask(src, d)
+    return m, bin(m).count("1")
+
+
+def rank_program(g, core, T, topo):
+    cores = list(T.cores)
+    plan = _plan(cores, topo)
+    rank = T.rank_of(core)
+    sem = T.sem
+    lands = [(p, k0, k1, "s%d_%d" % (p, k0), _mask(topo, s, ds)[1]) for (p, k0, k1, s, ds) in plan if core in ds]
+    mine = [e for e in plan if e[3] == core]
+    if rank is None:
+        return
+
+    def cols(k0, k1):
+        return slice(k0 * RW, k1 * RW)
+
+    if rank < NP_:
+        h = T["l%d" % rank]
+        g.sync.dma_start(T.xs[:], T.x[:]).then_inc(sem.ld, 16)
+        g.scalar.dma_start(T.w1s[:], T.w1[:]).then_inc(sem.ld, 16)
+        g.vector.memset(T.zero[:], 0.0).then_inc(sem.z, 1)
+        g.tensor.wait_ge(sem.ld, 32)
+        for k in range(NR):
+            g.tensor.matmul(T["pb%d" % k][:, 0:RW], T.w1s[:], T.xs[:, cols(k, k + 1)], True, True).then_inc(sem["mm%d" % k], 1)
+        g.vector.wait_ge(sem.z, 1)
+        for k in range(NR):
+            g.vector.wait_ge(sem["mm%d" % k], 1)
+            g.vector.tensor_tensor(h[:, cols(k, k + 1)], T["pb%d" % k][:, 0:RW], T.zero[:], AluOpType.max).then_inc(sem["v%d" % k], 1)
+
+    waited, sent = set(), 0
+    for (p, k0, k1, _s, dsts) in mine:
+        if cores[p] == core:
+            need = [("v%d" % k, 1) for k in range(k0, k1)]
+        else:
+            need = [(s, n) for (lp, a, b, s, n) in lands if lp == p and a < k1 and k0 < b]
+        for s, n in need:
+            if s not in waited:
+                g.wait_ge(sem[s], n)
+                waited.add(s)
+        buf = T["l%d" % p][:, cols(k0, k1)]
+        m, n = _mask(topo, core, dsts)
+        arrive = sem["s%d_%d" % (p, k0)]
+        if len(dsts) == 1:
+            rid, pid = topo.addr(dsts[0], core)
+            g.remote_dma(buf, buf, arrive, sem.sent, pid, rid, m)
+        else:
+            ids = [DstId(rid=a[0], pnc=a[1]) for a in (topo.addr(d, core) for d in dsts)]
+            g.remote_dma_fused([RemoteDMATransfer(dst_ids=ids, dma_engine_mask=m, remote_sem=arrive, src=buf,
+                                                  dsts=[buf for _ in dsts])], local_sem=sem.sent)
+        sent += n
+    if sent:
+        g.wait_ge(sem.sent, sent)
+
+    if rank >= NP_:
+        g.sync.dma_start(T.w2s[:], T.w2[:]).then_inc(sem.ld, 16)
+        g.tensor.wait_ge(sem.ld, 16)
+        seen, order = [0] * NR, []
+        for (p, k0, k1, s, n) in lands:
+            g.tensor.wait_ge(sem[s], n)
+            for k in range(k0, k1):
+                seen[k] += 1
+                ins = g.tensor.matmul(T["pb%d" % k][:, 0:RW], T.w2s[:, p * D:(p + 1) * D], T["l%d" % p][:, cols(k, k + 1)],
+                                      seen[k] == 1, seen[k] == NP_)
+                if seen[k] == NP_:
+                    ins.then_inc(sem["mm%d" % k], 1)
+                    order.append(k)
+        for k in order:
+            g.vector.wait_ge(sem["mm%d" % k], 1)
+            g.vector.tensor_copy(T.ys[:, cols(k, k + 1)], T["pb%d" % k][:, 0:RW]).then_inc(sem["v%d" % k], 1)
+        queues = [g.sync, g.scalar]
+        for i, k in enumerate(order):
+            q = queues[i % 2]
+            q.wait_ge(sem["v%d" % k], 1)
+            q.dma_start(T.y[:, cols(k, k + 1)], T.ys[:, cols(k, k + 1)]).then_inc(sem["st%d" % k], 16)
+        for i, k in enumerate(order):
+            queues[i % 2].wait_ge(sem["st%d" % k], 16)

@@ -22,28 +22,41 @@ SEMAPHORES += ["mm%d" % _k for _k in range(NR)] + ["v%d" % _k for _k in range(NR
 SEMAPHORES += ["s%d_%d" % (_p, _k) for _p in range(NP_) for _k in range(NR)]
 
 
+def _rack(topo, c):
+    return topo.rack(topo.host(c))
+
+
 def _plan(cores, topo):
     P, Q = cores[:NP_], cores[NP_:]
     first, direct, second = [], [], []
     for p, src in enumerate(P):
-        near = [q for q in Q if topo.may_write(src, q)]
+        near = sorted((q for q in Q if topo.may_write(src, q)), key=lambda q: _rack(topo, q) == _rack(topo, src))
         far = [q for q in Q if not topo.may_write(src, q)]
         if near:
-            direct.append((p, 0, NR, src, near))
+            if far:
+                direct.append((p, 0, NR, src, near, None))
+            else:
+                direct += [(p, k, k + 1, src, near, k) for k in range(NR)]
         if far:
             relays = [r for r in P if r != src and topo.may_write(src, r) and all(topo.may_write(r, q) for q in far)]
+            there = [r for r in relays if all(_rack(topo, r) == _rack(topo, q) for q in far)]
+            relays = there or relays
             for k in range(NR):
                 r = relays[k * len(relays) // NR]
-                first.append((p, k, k + 1, src, [r]))
-                second.append((p, k, k + 1, r, far))
+                first.append((p, k, k + 1, src, [r], k))
+                second.append((p, k, k + 1, r, far, None))
     return first + direct + second
 
 
-def _mask(topo, src, dsts):
+def _mask(topo, src, dsts, part):
     m = topo.mask(src, dsts[0])
     for d in dsts[1:]:
         m &= topo.mask(src, d)
-    return m, bin(m).count("1")
+    bits = [i for i in range(m.bit_length()) if (m >> i) & 1]
+    if part is not None:
+        n = len(bits) // NR
+        bits = bits[part * n:(part + 1) * n]
+    return sum(1 << i for i in bits), len(bits)
 
 
 def rank_program(g, core, T, topo):
@@ -51,7 +64,7 @@ def rank_program(g, core, T, topo):
     plan = _plan(cores, topo)
     rank = T.rank_of(core)
     sem = T.sem
-    lands = [(p, k0, k1, "s%d_%d" % (p, k0), _mask(topo, s, ds)[1]) for (p, k0, k1, s, ds) in plan if core in ds]
+    lands = [(p, k0, k1, "s%d_%d" % (p, k0), _mask(topo, s, ds, pt)[1]) for (p, k0, k1, s, ds, pt) in plan if core in ds]
     mine = [e for e in plan if e[3] == core]
     if rank is None:
         return
@@ -73,7 +86,7 @@ def rank_program(g, core, T, topo):
             g.vector.tensor_tensor(h[:, cols(k, k + 1)], T["pb%d" % k][:, 0:RW], T.zero[:], AluOpType.max).then_inc(sem["v%d" % k], 1)
 
     waited, sent = set(), 0
-    for (p, k0, k1, _s, dsts) in mine:
+    for (p, k0, k1, _s, dsts, part) in mine:
         if cores[p] == core:
             need = [("v%d" % k, 1) for k in range(k0, k1)]
         else:
@@ -83,7 +96,7 @@ def rank_program(g, core, T, topo):
                 g.wait_ge(sem[s], n)
                 waited.add(s)
         buf = T["l%d" % p][:, cols(k0, k1)]
-        m, n = _mask(topo, core, dsts)
+        m, n = _mask(topo, core, dsts, part)
         arrive = sem["s%d_%d" % (p, k0)]
         if len(dsts) == 1:
             rid, pid = topo.addr(dsts[0], core)

@@ -2,14 +2,15 @@ from concourse.bass import DstId, RemoteDMATransfer
 from concourse.mybir import AluOpType
 
 NP_, TK, D = 3, 512, 128
-NR = 2
-RW = TK // NR
+EDGE = [0, 128, 384, 512]
+NR = len(EDGE) - 1
+WID = [EDGE[_k + 1] - EDGE[_k] for _k in range(NR)]
 
 SCRATCH = {
     "xs": ("sbuf", [D, TK], "bfloat16"),
     "w1s": ("sbuf", [D, D], "bfloat16"),
     "w2s": ("sbuf", [D, NP_ * D], "bfloat16"),
-    "zero": ("sbuf", [D, RW], "bfloat16"),
+    "zero": ("sbuf", [D, max(WID)], "bfloat16"),
     "ys": ("sbuf", [D, TK], "bfloat16"),
 }
 for _p in range(NP_):
@@ -28,24 +29,28 @@ def _rack(topo, c):
 
 def _plan(cores, topo):
     P, Q = cores[:NP_], cores[NP_:]
-    first, direct, second = [], [], []
+    haul, direct, pass_on = [[] for _ in range(NR)], [], [[] for _ in range(NR)]
     for p, src in enumerate(P):
-        near = sorted((q for q in Q if topo.may_write(src, q)), key=lambda q: _rack(topo, q) == _rack(topo, src))
+        near = [q for q in Q if topo.may_write(src, q)]
         far = [q for q in Q if not topo.may_write(src, q)]
-        if near:
-            if far:
-                direct.append((p, 0, NR, src, near, None))
-            else:
-                direct += [(p, k, k + 1, src, near, k) for k in range(NR)]
+        home = [q for q in near if _rack(topo, q) == _rack(topo, src)]
+        away = [q for q in near if q not in home]
+        if home:
+            direct.append((p, 0, NR, src, home, 1))
+        if away:
+            head = ([q for q in away if topo.chip(q) == topo.chip(src)] + away)[0]
+            rest = [q for q in away if q != head]
+            for k in range(NR):
+                haul[k].append((p, k, k + 1, src, [head], 0))
+                if rest:
+                    pass_on[k].append((p, k, k + 1, head, rest, 1))
         if far:
             relays = [r for r in P if r != src and topo.may_write(src, r) and all(topo.may_write(r, q) for q in far)]
-            there = [r for r in relays if all(_rack(topo, r) == _rack(topo, q) for q in far)]
-            relays = there or relays
+            r = ([r for r in relays if all(_rack(topo, r) == _rack(topo, q) for q in far)] + relays)[0]
             for k in range(NR):
-                r = relays[k * len(relays) // NR]
-                first.append((p, k, k + 1, src, [r], k))
-                second.append((p, k, k + 1, r, far, None))
-    return first + direct + second
+                haul[k].append((p, k, k + 1, src, [r], 0))
+                pass_on[k].append((p, k, k + 1, r, far, 1 if k == 0 else None))
+    return [e for st in haul for e in st] + direct + [e for st in pass_on for e in st]
 
 
 def _mask(topo, src, dsts, part):
@@ -54,8 +59,7 @@ def _mask(topo, src, dsts, part):
         m &= topo.mask(src, d)
     bits = [i for i in range(m.bit_length()) if (m >> i) & 1]
     if part is not None:
-        n = len(bits) // NR
-        bits = bits[part * n:(part + 1) * n]
+        bits = bits[1 - part::2]
     return sum(1 << i for i in bits), len(bits)
 
 
@@ -70,7 +74,7 @@ def rank_program(g, core, T, topo):
         return
 
     def cols(k0, k1):
-        return slice(k0 * RW, k1 * RW)
+        return slice(EDGE[k0], EDGE[k1])
 
     if rank < NP_:
         h = T["l%d" % rank]
@@ -79,11 +83,12 @@ def rank_program(g, core, T, topo):
         g.vector.memset(T.zero[:], 0.0).then_inc(sem.z, 1)
         g.tensor.wait_ge(sem.ld, 32)
         for k in range(NR):
-            g.tensor.matmul(T["pb%d" % k][:, 0:RW], T.w1s[:], T.xs[:, cols(k, k + 1)], True, True).then_inc(sem["mm%d" % k], 1)
+            g.tensor.matmul(T["pb%d" % k][:, 0:WID[k]], T.w1s[:], T.xs[:, cols(k, k + 1)], True, True).then_inc(sem["mm%d" % k], 1)
         g.vector.wait_ge(sem.z, 1)
         for k in range(NR):
             g.vector.wait_ge(sem["mm%d" % k], 1)
-            g.vector.tensor_tensor(h[:, cols(k, k + 1)], T["pb%d" % k][:, 0:RW], T.zero[:], AluOpType.max).then_inc(sem["v%d" % k], 1)
+            g.vector.tensor_tensor(h[:, cols(k, k + 1)], T["pb%d" % k][:, 0:WID[k]], T.zero[:, 0:WID[k]],
+                                   AluOpType.max).then_inc(sem["v%d" % k], 1)
 
     waited, sent = set(), 0
     for (p, k0, k1, _s, dsts, part) in mine:
@@ -117,14 +122,14 @@ def rank_program(g, core, T, topo):
             g.tensor.wait_ge(sem[s], n)
             for k in range(k0, k1):
                 seen[k] += 1
-                ins = g.tensor.matmul(T["pb%d" % k][:, 0:RW], T.w2s[:, p * D:(p + 1) * D], T["l%d" % p][:, cols(k, k + 1)],
+                ins = g.tensor.matmul(T["pb%d" % k][:, 0:WID[k]], T.w2s[:, p * D:(p + 1) * D], T["l%d" % p][:, cols(k, k + 1)],
                                       seen[k] == 1, seen[k] == NP_)
                 if seen[k] == NP_:
                     ins.then_inc(sem["mm%d" % k], 1)
                     order.append(k)
         for k in order:
             g.vector.wait_ge(sem["mm%d" % k], 1)
-            g.vector.tensor_copy(T.ys[:, cols(k, k + 1)], T["pb%d" % k][:, 0:RW]).then_inc(sem["v%d" % k], 1)
+            g.vector.tensor_copy(T.ys[:, cols(k, k + 1)], T["pb%d" % k][:, 0:WID[k]]).then_inc(sem["v%d" % k], 1)
         queues = [g.sync, g.scalar]
         for i, k in enumerate(order):
             q = queues[i % 2]

@@ -2,8 +2,9 @@ from concourse.bass import DstId, RemoteDMATransfer
 from concourse.mybir import AluOpType
 
 NP_, TK, D = 3, 512, 128
-EDGE = [0, 128, 384, 512]
+EDGE = [0, 128, 256, 384, 512]
 NR = len(EDGE) - 1
+SIDE = NR - 1
 WID = [EDGE[_k + 1] - EDGE[_k] for _k in range(NR)]
 
 SCRATCH = {
@@ -27,30 +28,61 @@ def _rack(topo, c):
     return topo.rack(topo.host(c))
 
 
+def _carrier(topo, cores, src, home, q, used):
+    for m in home:
+        if topo.chip(m) == topo.chip(q) and topo.may_write(m, q) and m not in used:
+            return m
+    for a in cores:
+        if _rack(topo, a) == _rack(topo, src) and topo.chip(a) == topo.chip(q) and topo.may_write(a, q):
+            for c in range(max(a - 7, 0), a + 8):
+                if (topo.host(c) == topo.host(a) and topo.chip(c) == topo.chip(a) and topo.die(c) != topo.die(a)
+                        and c not in cores and c not in used and topo.may_write(src, c) and topo.may_write(c, q)):
+                    return c
+    return None
+
+
 def _plan(cores, topo):
     P, Q = cores[:NP_], cores[NP_:]
-    haul, direct, pass_on = [[] for _ in range(NR)], [], [[] for _ in range(NR)]
+    first, haul, tail, direct, side_on, pass_on = [], [[], []], [], [], [], [[], []]
+    used = set()
     for p, src in enumerate(P):
         near = [q for q in Q if topo.may_write(src, q)]
         far = [q for q in Q if not topo.may_write(src, q)]
         home = [q for q in near if _rack(topo, q) == _rack(topo, src)]
         away = [q for q in near if q not in home]
-        if home:
-            direct.append((p, 0, NR, src, home, 1))
+        groups = []
         if away:
             head = ([q for q in away if topo.chip(q) == topo.chip(src)] + away)[0]
-            rest = [q for q in away if q != head]
-            for k in range(NR):
-                haul[k].append((p, k, k + 1, src, [head], 0))
-                if rest:
-                    pass_on[k].append((p, k, k + 1, head, rest, 1))
+            groups.append((head, [q for q in away if q != head], True))
         if far:
             relays = [r for r in P if r != src and topo.may_write(src, r) and all(topo.may_write(r, q) for q in far)]
-            r = ([r for r in relays if all(_rack(topo, r) == _rack(topo, q) for q in far)] + relays)[0]
-            for k in range(NR):
-                haul[k].append((p, k, k + 1, src, [r], 0))
-                pass_on[k].append((p, k, k + 1, r, far, 1 if k == 0 else None))
-    return [e for st in haul for e in st] + direct + [e for st in pass_on for e in st]
+            groups.append((([r for r in relays if all(_rack(topo, r) == _rack(topo, q) for q in far)] + relays)[0], far, False))
+        early = []
+        for mid, targets, keeps in groups:
+            carry = []
+            for q in targets:
+                c = _carrier(topo, cores, src, home, q, used)
+                carry.append(c)
+                used.add(c)
+            main = NR if None in carry else SIDE
+            cut = 1 if keeps else main - 1
+            for i, (a, b) in enumerate([(0, cut), (cut, main)]):
+                haul[i].append((p, a, b, src, [mid], 0))
+                if targets:
+                    pass_on[i].append((p, a, b, mid, targets, 1 if keeps else None))
+            if main < NR:
+                if keeps:
+                    tail.append((p, SIDE, NR, src, [mid], 0))
+                for c, q in zip(carry, targets):
+                    early.append(c)
+                    side_on.append((p, SIDE, NR, c, [q], 2))
+        split = any(c in home for c in early)
+        early = (home if split else []) + [c for c in early if c not in home]
+        if early:
+            first.append((p, SIDE, NR, src, early, 1))
+        if home:
+            direct.append((p, 0, SIDE if split else NR, src, home, 1))
+    return first + haul[0] + haul[1] + tail + direct + pass_on[0] + side_on + pass_on[1]
 
 
 def _mask(topo, src, dsts, part):
@@ -58,7 +90,9 @@ def _mask(topo, src, dsts, part):
     for d in dsts[1:]:
         m &= topo.mask(src, d)
     bits = [i for i in range(m.bit_length()) if (m >> i) & 1]
-    if part is not None:
+    if part == 2:
+        bits = bits[1::4]
+    elif part is not None:
         bits = bits[1 - part::2]
     return sum(1 << i for i in bits), len(bits)
 
@@ -70,22 +104,25 @@ def rank_program(g, core, T, topo):
     sem = T.sem
     lands = [(p, k0, k1, "s%d_%d" % (p, k0), _mask(topo, s, ds, pt)[1]) for (p, k0, k1, s, ds, pt) in plan if core in ds]
     mine = [e for e in plan if e[3] == core]
-    if rank is None:
+    if rank is None and not mine:
         return
 
     def cols(k0, k1):
         return slice(EDGE[k0], EDGE[k1])
 
-    if rank < NP_:
+    if rank is not None and rank < NP_:
         h = T["l%d" % rank]
+        turn = []
+        for e in mine:
+            turn += [k for k in range(e[1], e[2]) if cores[e[0]] == core and k not in turn]
         g.sync.dma_start(T.xs[:], T.x[:]).then_inc(sem.ld, 16)
         g.scalar.dma_start(T.w1s[:], T.w1[:]).then_inc(sem.ld, 16)
         g.vector.memset(T.zero[:], 0.0).then_inc(sem.z, 1)
         g.tensor.wait_ge(sem.ld, 32)
-        for k in range(NR):
+        for k in turn:
             g.tensor.matmul(T["pb%d" % k][:, 0:WID[k]], T.w1s[:], T.xs[:, cols(k, k + 1)], True, True).then_inc(sem["mm%d" % k], 1)
         g.vector.wait_ge(sem.z, 1)
-        for k in range(NR):
+        for k in turn:
             g.vector.wait_ge(sem["mm%d" % k], 1)
             g.vector.tensor_tensor(h[:, cols(k, k + 1)], T["pb%d" % k][:, 0:WID[k]], T.zero[:, 0:WID[k]],
                                    AluOpType.max).then_inc(sem["v%d" % k], 1)
@@ -114,7 +151,7 @@ def rank_program(g, core, T, topo):
     if sent:
         g.wait_ge(sem.sent, sent)
 
-    if rank >= NP_:
+    if rank is not None and rank >= NP_:
         g.sync.dma_start(T.w2s[:], T.w2[:]).then_inc(sem.ld, 16)
         g.tensor.wait_ge(sem.ld, 16)
         seen, order = [0] * NR, []

from concourse.bass import DstId, RemoteDMATransfer
from concourse.mybir import AluOpType

NP_, TK, D = 3, 512, 128
EDGE = [0, 128, 256, 384, 512]
NR = len(EDGE) - 1
SIDE = NR - 1
WID = [EDGE[_k + 1] - EDGE[_k] for _k in range(NR)]

SCRATCH = {
    "xs": ("sbuf", [D, TK], "bfloat16"),
    "w1s": ("sbuf", [D, D], "bfloat16"),
    "w2s": ("sbuf", [D, NP_ * D], "bfloat16"),
    "zero": ("sbuf", [D, max(WID)], "bfloat16"),
    "ys": ("sbuf", [D, TK], "bfloat16"),
}
for _p in range(NP_):
    SCRATCH["l%d" % _p] = ("sbuf", [D, TK], "bfloat16")
for _k in range(NR):
    SCRATCH["pb%d" % _k] = ("psum", [D, 512], "float32")

SEMAPHORES = ["ld", "z", "sent"]
SEMAPHORES += ["mm%d" % _k for _k in range(NR)] + ["v%d" % _k for _k in range(NR)] + ["st%d" % _k for _k in range(NR)]
SEMAPHORES += ["s%d_%d" % (_p, _k) for _p in range(NP_) for _k in range(NR)]


def _rack(topo, c):
    return topo.rack(topo.host(c))


def _carrier(topo, cores, src, home, q, used):
    for m in home:
        if topo.chip(m) == topo.chip(q) and topo.may_write(m, q) and m not in used:
            return m
    for a in cores:
        if _rack(topo, a) == _rack(topo, src) and topo.chip(a) == topo.chip(q) and topo.may_write(a, q):
            for c in range(max(a - 7, 0), a + 8):
                if (topo.host(c) == topo.host(a) and topo.chip(c) == topo.chip(a) and topo.die(c) != topo.die(a)
                        and c not in cores and c not in used and topo.may_write(src, c) and topo.may_write(c, q)):
                    return c
    return None


def _plan(cores, topo):
    P, Q = cores[:NP_], cores[NP_:]
    first, haul, tail, direct, side_on, pass_on = [], [[], []], [], [], [], [[], []]
    used = set()
    for p, src in enumerate(P):
        near = [q for q in Q if topo.may_write(src, q)]
        far = [q for q in Q if not topo.may_write(src, q)]
        home = [q for q in near if _rack(topo, q) == _rack(topo, src)]
        away = [q for q in near if q not in home]
        groups = []
        if away:
            head = ([q for q in away if topo.chip(q) == topo.chip(src)] + away)[0]
            groups.append((head, [q for q in away if q != head], True))
        if far:
            relays = [r for r in P if r != src and topo.may_write(src, r) and all(topo.may_write(r, q) for q in far)]
            groups.append((([r for r in relays if all(_rack(topo, r) == _rack(topo, q) for q in far)] + relays)[0], far, False))
        early = []
        for mid, targets, keeps in groups:
            carry = []
            for q in targets:
                c = _carrier(topo, cores, src, home, q, used)
                carry.append(c)
                used.add(c)
            main = NR if None in carry else SIDE
            cut = 1 if keeps else main - 1
            for i, (a, b) in enumerate([(0, cut), (cut, main)]):
                haul[i].append((p, a, b, src, [mid], 0))
                if targets:
                    pass_on[i].append((p, a, b, mid, targets, 1 if keeps else None))
            if main < NR:
                if keeps:
                    tail.append((p, SIDE, NR, src, [mid], 0))
                for c, q in zip(carry, targets):
                    early.append(c)
                    side_on.append((p, SIDE, NR, c, [q], 2))
        split = any(c in home for c in early)
        early = (home if split else []) + [c for c in early if c not in home]
        if early:
            first.append((p, SIDE, NR, src, early, 1))
        if home:
            direct.append((p, 0, SIDE if split else NR, src, home, 1))
    return first + haul[0] + haul[1] + tail + direct + pass_on[0] + side_on + pass_on[1]


def _mask(topo, src, dsts, part):
    m = topo.mask(src, dsts[0])
    for d in dsts[1:]:
        m &= topo.mask(src, d)
    bits = [i for i in range(m.bit_length()) if (m >> i) & 1]
    if part == 2:
        bits = bits[1::4]
    elif part is not None:
        bits = bits[1 - part::2]
    return sum(1 << i for i in bits), len(bits)


def rank_program(g, core, T, topo):
    cores = list(T.cores)
    plan = _plan(cores, topo)
    rank = T.rank_of(core)
    sem = T.sem
    lands = [(p, k0, k1, "s%d_%d" % (p, k0), _mask(topo, s, ds, pt)[1]) for (p, k0, k1, s, ds, pt) in plan if core in ds]
    mine = [e for e in plan if e[3] == core]
    if rank is None and not mine:
        return

    def cols(k0, k1):
        return slice(EDGE[k0], EDGE[k1])

    if rank is not None and rank < NP_:
        h = T["l%d" % rank]
        turn = []
        for e in mine:
            turn += [k for k in range(e[1], e[2]) if cores[e[0]] == core and k not in turn]
        g.sync.dma_start(T.xs[:], T.x[:]).then_inc(sem.ld, 16)
        g.scalar.dma_start(T.w1s[:], T.w1[:]).then_inc(sem.ld, 16)
        g.vector.memset(T.zero[:], 0.0).then_inc(sem.z, 1)
        g.tensor.wait_ge(sem.ld, 32)
        for k in turn:
            g.tensor.matmul(T["pb%d" % k][:, 0:WID[k]], T.w1s[:], T.xs[:, cols(k, k + 1)], True, True).then_inc(sem["mm%d" % k], 1)
        g.vector.wait_ge(sem.z, 1)
        for k in turn:
            g.vector.wait_ge(sem["mm%d" % k], 1)
            g.vector.tensor_tensor(h[:, cols(k, k + 1)], T["pb%d" % k][:, 0:WID[k]], T.zero[:, 0:WID[k]],
                                   AluOpType.max).then_inc(sem["v%d" % k], 1)

    waited, sent = set(), 0
    for (p, k0, k1, _s, dsts, part) in mine:
        if cores[p] == core:
            need = [("v%d" % k, 1) for k in range(k0, k1)]
        else:
            need = [(s, n) for (lp, a, b, s, n) in lands if lp == p and a < k1 and k0 < b]
        for s, n in need:
            if s not in waited:
                g.wait_ge(sem[s], n)
                waited.add(s)
        buf = T["l%d" % p][:, cols(k0, k1)]
        m, n = _mask(topo, core, dsts, part)
        arrive = sem["s%d_%d" % (p, k0)]
        if len(dsts) == 1:
            rid, pid = topo.addr(dsts[0], core)
            g.remote_dma(buf, buf, arrive, sem.sent, pid, rid, m)
        else:
            ids = [DstId(rid=a[0], pnc=a[1]) for a in (topo.addr(d, core) for d in dsts)]
            g.remote_dma_fused([RemoteDMATransfer(dst_ids=ids, dma_engine_mask=m, remote_sem=arrive, src=buf,
                                                  dsts=[buf for _ in dsts])], local_sem=sem.sent)
        sent += n
    if sent:
        g.wait_ge(sem.sent, sent)

    if rank is not None and rank >= NP_:
        g.sync.dma_start(T.w2s[:], T.w2[:]).then_inc(sem.ld, 16)
        g.tensor.wait_ge(sem.ld, 16)
        seen, order = [0] * NR, []
        for (p, k0, k1, s, n) in lands:
            g.tensor.wait_ge(sem[s], n)
            for k in range(k0, k1):
                seen[k] += 1
                ins = g.tensor.matmul(T["pb%d" % k][:, 0:WID[k]], T.w2s[:, p * D:(p + 1) * D], T["l%d" % p][:, cols(k, k + 1)],
                                      seen[k] == 1, seen[k] == NP_)
                if seen[k] == NP_:
                    ins.then_inc(sem["mm%d" % k], 1)
                    order.append(k)
        for k in order:
            g.vector.wait_ge(sem["mm%d" % k], 1)
            g.vector.tensor_copy(T.ys[:, cols(k, k + 1)], T["pb%d" % k][:, 0:WID[k]]).then_inc(sem["v%d" % k], 1)
        queues = [g.sync, g.scalar]
        for i, k in enumerate(order):
            q = queues[i % 2]
            q.wait_ge(sem["v%d" % k], 1)
            q.dma_start(T.y[:, cols(k, k + 1)], T.ys[:, cols(k, k + 1)]).then_inc(sem["st%d" % k], 16)
        for i, k in enumerate(order):
            queues[i % 2].wait_ge(sem["st%d" % k], 16)
